import numpy as np, ml_dtypes
CORES = [5,29,101,125,133,157,229,253]
N = 8
KT, C = 8, 64
def setup_inputs(rng):
    return {"x": rng.standard_normal((N, 128, KT * C), dtype=np.float32).astype(ml_dtypes.bfloat16)}
def setup_inputs_big(rng):
    d = setup_inputs(rng)
    for k in ("x",): d[k] = (d[k].astype(np.float32) * 1024.0).astype(d[k].dtype)
    return d
def setup_inputs_small(rng):
    d = setup_inputs(rng)
    for k in ("x",): d[k] = (d[k].astype(np.float32) * (1 / 1024.0)).astype(d[k].dtype)
    return d
def setup_inputs_apart(rng):
    d = setup_inputs(rng)
    f = (10.0 ** rng.permutation(np.linspace(-1.5, 1.5, N))).astype(np.float32).reshape(N, 1, 1)
    for k in ("x",): d[k] = (d[k].astype(np.float32) * f).astype(d[k].dtype)
    return d
def reference(x):
    X = x.astype(np.float64)
    y = np.full((N, C, N * C), np.nan)
    for r in range(N):
        for i in range(N):
            s = i
            if s != r: y[r][:, C * i:C * i + C] = sum(X[r][:, C * t:C * t + C].T @ X[s][:, C * t:C * t + C] for t in range(KT))
    return {"y": y.astype(ml_dtypes.bfloat16 if x.dtype != np.float64 else np.float64)}

@@ -1,0 +1,181 @@
+from concourse.bass import DstId, RemoteDMATransfer
+from concourse.mybir import AluOpType
+
+SIM_CORES = 256
+KT, C = 8, 64
+W = KT * C
+H = W // 2
+HT = KT // 2
+
+SCRATCH = {
+    "xs": ("sbuf", [128, W], "bfloat16"),
+    "xn": ("sbuf", [128, W], "bfloat16"),
+    "xh": ("sbuf", [128, H], "bfloat16"),
+    "xc": ("sbuf", [128, 4 * W], "bfloat16"),
+    "ys": ("sbuf", [128, 8 * C], "bfloat16"),
+    "ret": ("sbuf", [128, 2 * C], "bfloat16"),
+    "part": ("sbuf", [128, C], "bfloat16"),
+    "pret": ("psum", [128, 512], "float32"),
+    "pkeep": ("psum", [128, 512], "float32"),
+    "pc0": ("psum", [128, 512], "float32"),
+    "pc1": ("psum", [128, 512], "float32"),
+    "pc2": ("psum", [128, 512], "float32"),
+    "pc3": ("psum", [128, 512], "float32"),
+}
+SEMAPHORES = ["ld", "hs", "an", "ao", "c0", "c1", "c2", "c3", "yr", "pr", "mret", "mkeep",
+              "mc0", "mc1", "mc2", "mc3", "vret", "vys", "ms", "st"]
+
+
+def _bits(mask):
+    return [1 << b for b in range(mask.bit_length()) if (mask >> b) & 1]
+
+
+def _join(bits):
+    m = 0
+    for b in bits:
+        m |= b
+    return m
+
+
+def _dst(topo, dst, src):
+    rid, pid = topo.addr(dst, src)
+    return DstId(rid=rid, pnc=pid)
+
+
+def _plan(rc, T, topo):
+    own = [c for c in T.cores if c == rc or topo.same_plane(c, rc)]
+    far = [c for c in T.cores if c not in own]
+    i = own.index(rc)
+    chip = [c for c in range(SIM_CORES) if topo.host(c) == topo.host(rc) and topo.chip(c) == topo.chip(rc)]
+    owners = [c for c in chip if c != rc and topo.may_write(c, far[0])]
+    near = [c for c in owners if topo.die(c) == topo.die(rc)]
+    away = [c for c in owners if topo.die(c) != topo.die(rc)]
+    jobs = []
+    for q, grp in enumerate((near, away)):
+        peers = [far[(i + 2 * q + k) % len(far)] for k in range(2)]
+        for h, c in enumerate(grp[:2]):
+            jobs.append((c, q, h, peers))
+    return own, far, i, jobs
+
+
+def _owner_program(g, core, T, topo, rc):
+    S = T.sem
+    own, far, i, jobs = _plan(rc, T, topo)
+    for (c, q, h, peers) in jobs:
+        if c != core:
+            continue
+        got = len(_bits(topo.mask(rc, core))) // len(jobs)
+        mask = topo.mask(core, peers[0]) & topo.mask(core, peers[1])
+        slot = T.xc[:, W * i + H * h: W * i + H * h + H]
+        g.wait_ge(S.ao, got)
+        g.remote_dma_fused([RemoteDMATransfer(dst_ids=[_dst(topo, p, core) for p in peers], dma_engine_mask=mask,
+                                              remote_sem=S["c%d" % i], srcs=[T.xh[:]], dsts=[slot, slot], alu_op=0)],
+                           local_sem=S.hs)
+        g.wait_ge(S.hs, len(_bits(mask)))
+
+
+def rank_program(g, core, T, topo):
+    S = T.sem
+    rank = T.rank_of(core)
+    if rank is None:
+        home = [c for c in T.cores if topo.host(c) == topo.host(core) and topo.chip(c) == topo.chip(core)]
+        if home:
+            _owner_program(g, core, T, topo, home[0])
+        return
+
+    own, far, i, jobs = _plan(core, T, topo)
+    n = len(own)
+    nxt, prv, opp = own[(i + 1) % n], own[(i - 1) % n], own[(i + 2) % n]
+    myh = 0 if i < n // 2 else 1
+
+    def blk(c):
+        k = T.rank_of(c)
+        return slice(C * k, C * k + C)
+
+    def tile(buf, t):
+        return buf[:, C * t: C * t + C]
+
+    g.sync.dma_start(T.xs[:], T.x[:]).then_inc(S.ld, 16)
+
+    g.wait_ge(S.ld, 16)
+    sent = 0
+    bits = _bits(_join([]) | topo.mask(core, jobs[0][0]))
+    per = len(bits) // len(jobs)
+    trs = []
+    for (c, q, h, peers) in jobs:
+        m = _join(bits[q::2][per * h: per * h + per])
+        trs.append(RemoteDMATransfer(dst_ids=[_dst(topo, c, core)], dma_engine_mask=m, remote_sem=S.ao,
+                                     src=T.xs[:, H * h: H * h + H], dst=T.xh[:]))
+        sent += per
+    g.remote_dma_fused(trs, local_sem=S.hs)
+    mp = topo.mask(core, prv)
+    rid, pid = topo.addr(prv, core)
+    g.remote_dma(out_ap=T.xn[:], in_ap=T.xs[:], remote_sem=S.an, local_sem=S.hs, pid=pid, routing_id=rid,
+                 dma_engine_mask=mp)
+    sent += len(_bits(mp))
+    mo = topo.mask(core, opp)
+    rid, pid = topo.addr(opp, core)
+    oh = 1 - myh
+    g.remote_dma(out_ap=T.xh[:], in_ap=T.xs[:, H * oh: H * oh + H], remote_sem=S.ao, local_sem=S.hs, pid=pid,
+                 routing_id=rid, dma_engine_mask=mo)
+    sent += len(_bits(mo))
+    n_an, n_ao = len(_bits(topo.mask(nxt, core))), len(_bits(topo.mask(opp, core)))
+
+    te = g.tensor
+    te.wait_ge(S.ld, 16)
+    te.wait_ge(S.an, n_an)
+    for t in range(KT):
+        mm = te.matmul(T.pret[0:C, 0:C], tile(T.xn, t), tile(T.xs, t), t == 0, t == KT - 1)
+    mm.then_inc(S.mret, 1)
+    te.wait_ge(S.ao, n_ao)
+    for k in range(HT):
+        mm = te.matmul(T.pret[0:C, C:2 * C], tile(T.xh, k), tile(T.xs, HT * myh + k), k == 0, k == HT - 1)
+    mm.then_inc(S.mret, 1)
+    for t in range(KT):
+        mm = te.matmul(T.pkeep[0:C, 0:C], tile(T.xs, t), tile(T.xn, t), t == 0, t == KT - 1)
+    mm.then_inc(S.mkeep, 1)
+    for k in range(HT):
+        mm = te.matmul(T.pkeep[0:C, C:2 * C], tile(T.xs, HT * myh + k), tile(T.xh, k), k == 0, k == HT - 1)
+    mm.then_inc(S.mkeep, 1)
+    for j, s in enumerate(far):
+        owners_s = [c for (c, q, h, peers) in _plan(s, T, topo)[3] if core in peers]
+        te.wait_ge(S["c%d" % j], sum(len(_bits(topo.mask(c, core))) for c in owners_s))
+        for t in range(KT):
+            mm = te.matmul(T["pc%d" % j][0:C, 0:C], tile(T.xs, t), tile(T.xc, KT * j + t), t == 0, t == KT - 1)
+        mm.then_inc(S["mc%d" % j], 1)
+
+    ve = g.vector
+    ve.memset(T.ret[C:2 * C, :], 0.0).then_inc(S.ms, 1)
+    ve.memset(T.ys[0:C, blk(core)], 0.0).then_inc(S.vys, 1)
+    nys = 1
+    ve.wait_ge(S.mret, 2)
+    ve.tensor_copy(T.ret[0:C, :], T.pret[0:C, 0:2 * C]).then_inc(S.vret, 1)
+    ve.wait_ge(S.mkeep, 2)
+    ve.tensor_copy(T.ys[0:C, blk(nxt)], T.pkeep[0:C, 0:C]).then_inc(S.vys, 1)
+    nys += 1
+    for j, s in enumerate(far):
+        ve.wait_ge(S["mc%d" % j], 1)
+        ve.tensor_copy(T.ys[0:C, blk(s)], T["pc%d" % j][0:C, 0:C]).then_inc(S.vys, 1)
+        nys += 1
+
+    rb = _bits(topo.mask(core, nxt) & topo.mask(core, opp))
+    m_n, m_o = _join(rb[0::2]), _join(rb[1::2])
+    g.wait_ge(S.ms, 1)
+    g.wait_ge(S.vret, 1)
+    g.remote_dma_fused([
+        RemoteDMATransfer(dst_ids=[_dst(topo, nxt, core)], dma_engine_mask=m_n, remote_sem=S.yr,
+                          src=T.ret[:, 0:C], dst=T.ys[:, blk(core)]),
+        RemoteDMATransfer(dst_ids=[_dst(topo, opp, core)], dma_engine_mask=m_o, remote_sem=S.pr,
+                          src=T.ret[:, C:2 * C], dst=T.part[:]),
+    ], local_sem=S.hs)
+    sent += len(rb)
+    g.wait_ge(S.hs, sent)
+
+    ve.wait_ge(S.pr, len(rb[1::2]))
+    ve.tensor_tensor(T.ys[0:C, blk(opp)], T.pkeep[0:C, C:2 * C], T.part[0:C, :], AluOpType.add).then_inc(S.vys, 1)
+    nys += 1
+
+    g.sync.wait_ge(S.vys, nys)
+    g.sync.wait_ge(S.yr, len(rb[0::2]))
+    g.sync.dma_start(T.y[:], T.ys[0:C, :]).then_inc(S.st, 16)
+    g.sync.wait_ge(S.st, 16)

@@ -15,15 +15,17 @@ SCRATCH = {
     "ys": ("sbuf", [128, 8 * C], "bfloat16"),
     "ret": ("sbuf", [128, 2 * C], "bfloat16"),
     "part": ("sbuf", [128, C], "bfloat16"),
-    "pret": ("psum", [128, 512], "float32"),
-    "pkeep": ("psum", [128, 512], "float32"),
+    "prn": ("psum", [128, 512], "float32"),
+    "pkn": ("psum", [128, 512], "float32"),
+    "prp": ("psum", [128, 512], "float32"),
+    "pkp": ("psum", [128, 512], "float32"),
     "pc0": ("psum", [128, 512], "float32"),
     "pc1": ("psum", [128, 512], "float32"),
     "pc2": ("psum", [128, 512], "float32"),
     "pc3": ("psum", [128, 512], "float32"),
 }
-SEMAPHORES = ["ld", "hs", "an", "ao", "c0", "c1", "c2", "c3", "yr", "pr", "mret", "mkeep",
-              "mc0", "mc1", "mc2", "mc3", "vret", "vys", "ms", "st"]
+SEMAPHORES = ["ld", "hs", "an", "ao", "c0", "c1", "c2", "c3", "yr", "pr", "mrn", "mkn", "mrp", "mkp",
+              "mc0", "mc1", "mc2", "mc3", "vrn", "vrp", "vys", "ms", "st"]
 
 
 def _bits(mask):
@@ -87,6 +89,7 @@ def rank_program(g, core, T, topo):
     n = len(own)
     nxt, prv, opp = own[(i + 1) % n], own[(i - 1) % n], own[(i + 2) % n]
     myh = 0 if i < n // 2 else 1
+    sent = [0]
 
     def blk(c):
         k = T.rank_of(c)
@@ -95,51 +98,56 @@ def rank_program(g, core, T, topo):
     def tile(buf, t):
         return buf[:, C * t: C * t + C]
 
+    def count(src):
+        return len(_bits(topo.mask(src, core)))
+
+    def write(d, out_ap, in_ap, sem):
+        m = topo.mask(core, d)
+        rid, pid = topo.addr(d, core)
+        g.remote_dma(out_ap=out_ap, in_ap=in_ap, remote_sem=sem, local_sem=S.hs, pid=pid, routing_id=rid,
+                     dma_engine_mask=m)
+        sent[0] += len(_bits(m))
+
+    arrivals = []
+    for j, s in enumerate(far):
+        mine = [(c, peers.index(core)) for (c, q, h, peers) in _plan(s, T, topo)[3] if core in peers]
+        arrivals.append((mine[0][1], j, s, sum(count(c) for (c, k) in mine)))
+    arrivals.sort()
+
     g.sync.dma_start(T.xs[:], T.x[:]).then_inc(S.ld, 16)
 
     g.wait_ge(S.ld, 16)
-    sent = 0
-    bits = _bits(_join([]) | topo.mask(core, jobs[0][0]))
+    bits = _bits(topo.mask(core, jobs[0][0]))
     per = len(bits) // len(jobs)
     trs = []
     for (c, q, h, peers) in jobs:
         m = _join(bits[q::2][per * h: per * h + per])
         trs.append(RemoteDMATransfer(dst_ids=[_dst(topo, c, core)], dma_engine_mask=m, remote_sem=S.ao,
                                      src=T.xs[:, H * h: H * h + H], dst=T.xh[:]))
-        sent += per
+        sent[0] += per
     g.remote_dma_fused(trs, local_sem=S.hs)
-    mp = topo.mask(core, prv)
-    rid, pid = topo.addr(prv, core)
-    g.remote_dma(out_ap=T.xn[:], in_ap=T.xs[:], remote_sem=S.an, local_sem=S.hs, pid=pid, routing_id=rid,
-                 dma_engine_mask=mp)
-    sent += len(_bits(mp))
-    mo = topo.mask(core, opp)
-    rid, pid = topo.addr(opp, core)
     oh = 1 - myh
-    g.remote_dma(out_ap=T.xh[:], in_ap=T.xs[:, H * oh: H * oh + H], remote_sem=S.ao, local_sem=S.hs, pid=pid,
-                 routing_id=rid, dma_engine_mask=mo)
-    sent += len(_bits(mo))
-    n_an, n_ao = len(_bits(topo.mask(nxt, core))), len(_bits(topo.mask(opp, core)))
+    write(prv, T.xn[:], T.xs[:], S.an)
+    write(opp, T.xh[:], T.xs[:, H * oh: H * oh + H], S.ao)
 
     te = g.tensor
     te.wait_ge(S.ld, 16)
-    te.wait_ge(S.an, n_an)
+    te.wait_ge(S.an, count(nxt))
     for t in range(KT):
-        mm = te.matmul(T.pret[0:C, 0:C], tile(T.xn, t), tile(T.xs, t), t == 0, t == KT - 1)
-    mm.then_inc(S.mret, 1)
-    te.wait_ge(S.ao, n_ao)
-    for k in range(HT):
-        mm = te.matmul(T.pret[0:C, C:2 * C], tile(T.xh, k), tile(T.xs, HT * myh + k), k == 0, k == HT - 1)
-    mm.then_inc(S.mret, 1)
+        mm = te.matmul(T.prn[0:C, 0:C], tile(T.xn, t), tile(T.xs, t), t == 0, t == KT - 1)
+    mm.then_inc(S.mrn, 1)
     for t in range(KT):
-        mm = te.matmul(T.pkeep[0:C, 0:C], tile(T.xs, t), tile(T.xn, t), t == 0, t == KT - 1)
-    mm.then_inc(S.mkeep, 1)
+        mm = te.matmul(T.pkn[0:C, 0:C], tile(T.xs, t), tile(T.xn, t), t == 0, t == KT - 1)
+    mm.then_inc(S.mkn, 1)
+    te.wait_ge(S.ao, count(opp))
     for k in range(HT):
-        mm = te.matmul(T.pkeep[0:C, C:2 * C], tile(T.xs, HT * myh + k), tile(T.xh, k), k == 0, k == HT - 1)
-    mm.then_inc(S.mkeep, 1)
-    for j, s in enumerate(far):
-        owners_s = [c for (c, q, h, peers) in _plan(s, T, topo)[3] if core in peers]
-        te.wait_ge(S["c%d" % j], sum(len(_bits(topo.mask(c, core))) for c in owners_s))
+        mm = te.matmul(T.prp[0:C, 0:C], tile(T.xh, k), tile(T.xs, HT * myh + k), k == 0, k == HT - 1)
+    mm.then_inc(S.mrp, 1)
+    for k in range(HT):
+        mm = te.matmul(T.pkp[0:C, 0:C], tile(T.xs, HT * myh + k), tile(T.xh, k), k == 0, k == HT - 1)
+    mm.then_inc(S.mkp, 1)
+    for (turn, j, s, cnt) in arrivals:
+        te.wait_ge(S["c%d" % j], cnt)
         for t in range(KT):
             mm = te.matmul(T["pc%d" % j][0:C, 0:C], tile(T.xs, t), tile(T.xc, KT * j + t), t == 0, t == KT - 1)
         mm.then_inc(S["mc%d" % j], 1)
@@ -148,34 +156,30 @@ def rank_program(g, core, T, topo):
     ve.memset(T.ret[C:2 * C, :], 0.0).then_inc(S.ms, 1)
     ve.memset(T.ys[0:C, blk(core)], 0.0).then_inc(S.vys, 1)
     nys = 1
-    ve.wait_ge(S.mret, 2)
-    ve.tensor_copy(T.ret[0:C, :], T.pret[0:C, 0:2 * C]).then_inc(S.vret, 1)
-    ve.wait_ge(S.mkeep, 2)
-    ve.tensor_copy(T.ys[0:C, blk(nxt)], T.pkeep[0:C, 0:C]).then_inc(S.vys, 1)
+    ve.wait_ge(S.mrn, 1)
+    ve.tensor_copy(T.ret[0:C, 0:C], T.prn[0:C, 0:C]).then_inc(S.vrn, 1)
+    ve.wait_ge(S.mkn, 1)
+    ve.tensor_copy(T.ys[0:C, blk(nxt)], T.pkn[0:C, 0:C]).then_inc(S.vys, 1)
     nys += 1
-    for j, s in enumerate(far):
+    ve.wait_ge(S.mrp, 1)
+    ve.tensor_copy(T.ret[0:C, C:2 * C], T.prp[0:C, 0:C]).then_inc(S.vrp, 1)
+    for (turn, j, s, cnt) in arrivals:
         ve.wait_ge(S["mc%d" % j], 1)
         ve.tensor_copy(T.ys[0:C, blk(s)], T["pc%d" % j][0:C, 0:C]).then_inc(S.vys, 1)
         nys += 1
-
-    rb = _bits(topo.mask(core, nxt) & topo.mask(core, opp))
-    m_n, m_o = _join(rb[0::2]), _join(rb[1::2])
-    g.wait_ge(S.ms, 1)
-    g.wait_ge(S.vret, 1)
-    g.remote_dma_fused([
-        RemoteDMATransfer(dst_ids=[_dst(topo, nxt, core)], dma_engine_mask=m_n, remote_sem=S.yr,
-                          src=T.ret[:, 0:C], dst=T.ys[:, blk(core)]),
-        RemoteDMATransfer(dst_ids=[_dst(topo, opp, core)], dma_engine_mask=m_o, remote_sem=S.pr,
-                          src=T.ret[:, C:2 * C], dst=T.part[:]),
-    ], local_sem=S.hs)
-    sent += len(rb)
-    g.wait_ge(S.hs, sent)
-
-    ve.wait_ge(S.pr, len(rb[1::2]))
-    ve.tensor_tensor(T.ys[0:C, blk(opp)], T.pkeep[0:C, C:2 * C], T.part[0:C, :], AluOpType.add).then_inc(S.vys, 1)
+    ve.wait_ge(S.mkp, 1)
+    ve.wait_ge(S.pr, count(opp))
+    ve.tensor_tensor(T.ys[0:C, blk(opp)], T.pkp[0:C, 0:C], T.part[0:C, :], AluOpType.add).then_inc(S.vys, 1)
     nys += 1
 
+    g.wait_ge(S.ms, 1)
+    g.wait_ge(S.vrn, 1)
+    write(nxt, T.ys[:, blk(core)], T.ret[:, 0:C], S.yr)
+    g.wait_ge(S.vrp, 1)
+    write(opp, T.part[:], T.ret[:, C:2 * C], S.pr)
+    g.wait_ge(S.hs, sent[0])
+
     g.sync.wait_ge(S.vys, nys)
-    g.sync.wait_ge(S.yr, len(rb[0::2]))
+    g.sync.wait_ge(S.yr, count(prv))
     g.sync.dma_start(T.y[:], T.ys[0:C, :]).then_inc(S.st, 16)
     g.sync.wait_ge(S.st, 16)

@@ -6,12 +6,17 @@ KT, C = 8, 64
 W = KT * C
 H = W // 2
 HT = KT // 2
+Q = W // 4
+XR = 128 // 4
 
 SCRATCH = {
+    "xd": ("dram", [512, Q], "bfloat16"),
+    "xo": ("dram", [128, Q], "bfloat16"),
     "xs": ("sbuf", [128, W], "bfloat16"),
     "xn": ("sbuf", [128, W], "bfloat16"),
     "xh": ("sbuf", [128, H], "bfloat16"),
     "xc": ("sbuf", [128, 4 * W], "bfloat16"),
+    "idn": ("sbuf", [128, C], "bfloat16"),
     "ys": ("sbuf", [128, 8 * C], "bfloat16"),
     "ret": ("sbuf", [128, 2 * C], "bfloat16"),
     "part": ("sbuf", [128, C], "bfloat16"),
@@ -24,8 +29,8 @@ SCRATCH = {
     "pc2": ("psum", [128, 512], "float32"),
     "pc3": ("psum", [128, 512], "float32"),
 }
-SEMAPHORES = ["ld", "hs", "an", "ao", "c0", "c1", "c2", "c3", "yr", "pr", "mrn", "mkn", "mrp", "mkp",
-              "mc0", "mc1", "mc2", "mc3", "vrn", "vrp", "vys", "ms", "st"]
+SEMAPHORES = ["ld", "ldd", "hs", "an", "ao", "c0", "c1", "c2", "c3", "yr", "pr", "mrn", "mkn", "mrp", "mkp",
+              "mc0", "mc1", "mc2", "mc3", "vrn", "vrp", "vys", "ms", "ms1", "idn", "st"]
 
 
 def _bits(mask):
@@ -52,9 +57,9 @@ def _plan(rc, T, topo):
     owners = [c for c in chip if c != rc and topo.may_write(c, far[0])]
     near = [c for c in owners if topo.die(c) == topo.die(rc)]
     away = [c for c in owners if topo.die(c) != topo.die(rc)]
+    peers = [far[(i + k) % len(far)] for k in range(len(far))]
     jobs = []
     for q, grp in enumerate((near, away)):
-        peers = [far[(i + 2 * q + k) % len(far)] for k in range(2)]
         for h, c in enumerate(grp[:2]):
             jobs.append((c, q, h, peers))
     return own, far, i, jobs
@@ -66,12 +71,16 @@ def _owner_program(g, core, T, topo, rc):
     for (c, q, h, peers) in jobs:
         if c != core:
             continue
+        u = 2 * q + h
         got = len(_bits(topo.mask(rc, core))) // len(jobs)
-        mask = topo.mask(core, peers[0]) & topo.mask(core, peers[1])
-        slot = T.xc[:, W * i + H * h: W * i + H * h + H]
+        mask = topo.mask(core, peers[0])
+        for p in peers:
+            mask &= topo.mask(core, p)
+        slot = T.xc[:, W * i + Q * u: W * i + Q * u + Q]
         g.wait_ge(S.ao, got)
         g.remote_dma_fused([RemoteDMATransfer(dst_ids=[_dst(topo, p, core) for p in peers], dma_engine_mask=mask,
-                                              remote_sem=S["c%d" % i], srcs=[T.xh[:]], dsts=[slot, slot], alu_op=0)],
+                                              remote_sem=S["c%d" % i], srcs=[T.xo[:]], dsts=[slot for p in peers],
+                                              alu_op=0)],
                            local_sem=S.hs)
         g.wait_ge(S.hs, len(_bits(mask)))
 
@@ -110,67 +119,89 @@ def rank_program(g, core, T, topo):
 
     arrivals = []
     for j, s in enumerate(far):
-        mine = [(c, peers.index(core)) for (c, q, h, peers) in _plan(s, T, topo)[3] if core in peers]
-        arrivals.append((mine[0][1], j, s, sum(count(c) for (c, k) in mine)))
+        theirs = _plan(s, T, topo)[3]
+        arrivals.append((theirs[0][3].index(core), j, s, sum(count(c) for (c, q, h, peers) in theirs)))
     arrivals.sort()
 
-    g.sync.dma_start(T.xs[:], T.x[:]).then_inc(S.ld, 16)
+    g.sync.dma_start(T.xd[:], T.x[:]).then_inc(S.ldd, 16)
+    nld = 0
+    for u in range(4):
+        qu = g.scalar if u % 2 == 0 else g.sync
+        qu.dma_start(T.xs[:, Q * u: Q * u + Q], T.x[XR * u: XR * u + XR, :]).then_inc(S.ld, 16)
+        nld += 16
 
-    g.wait_ge(S.ld, 16)
+    g.wait_ge(S.ms1, 1)
+    g.affine_select(T.idn[0:C, :], T.idn[0:C, :], [[-1, C]], AluOpType.is_equal, 0.0, 0, 1).then_inc(S.idn, 1)
+    g.wait_ge(S.ldd, 16)
     bits = _bits(topo.mask(core, jobs[0][0]))
     per = len(bits) // len(jobs)
     trs = []
     for (c, q, h, peers) in jobs:
+        u = 2 * q + h
         m = _join(bits[q::2][per * h: per * h + per])
         trs.append(RemoteDMATransfer(dst_ids=[_dst(topo, c, core)], dma_engine_mask=m, remote_sem=S.ao,
-                                     src=T.xs[:, H * h: H * h + H], dst=T.xh[:]))
+                                     src=T.xd[128 * u: 128 * u + 128, :], dst=T.xo[:]))
         sent[0] += per
     g.remote_dma_fused(trs, local_sem=S.hs)
     oh = 1 - myh
+    g.wait_ge(S.ld, nld)
     write(prv, T.xn[:], T.xs[:], S.an)
     write(opp, T.xh[:], T.xs[:, H * oh: H * oh + H], S.ao)
 
     te = g.tensor
-    te.wait_ge(S.ld, 16)
-    te.wait_ge(S.an, count(nxt))
-    for t in range(KT):
-        mm = te.matmul(T.prn[0:C, 0:C], tile(T.xn, t), tile(T.xs, t), t == 0, t == KT - 1)
-    mm.then_inc(S.mrn, 1)
-    for t in range(KT):
-        mm = te.matmul(T.pkn[0:C, 0:C], tile(T.xs, t), tile(T.xn, t), t == 0, t == KT - 1)
-    mm.then_inc(S.mkn, 1)
-    te.wait_ge(S.ao, count(opp))
-    for k in range(HT):
-        mm = te.matmul(T.prp[0:C, 0:C], tile(T.xh, k), tile(T.xs, HT * myh + k), k == 0, k == HT - 1)
-    mm.then_inc(S.mrp, 1)
-    for k in range(HT):
-        mm = te.matmul(T.pkp[0:C, 0:C], tile(T.xs, HT * myh + k), tile(T.xh, k), k == 0, k == HT - 1)
-    mm.then_inc(S.mkp, 1)
-    for (turn, j, s, cnt) in arrivals:
+
+    def far_product(a):
+        (step, j, s, cnt) = a
         te.wait_ge(S["c%d" % j], cnt)
         for t in range(KT):
             mm = te.matmul(T["pc%d" % j][0:C, 0:C], tile(T.xs, t), tile(T.xc, KT * j + t), t == 0, t == KT - 1)
         mm.then_inc(S["mc%d" % j], 1)
 
+    te.wait_ge(S.ld, nld)
+    te.wait_ge(S.an, count(nxt))
+    for t in range(KT):
+        mm = te.matmul(T.prn[0:C, 0:C], tile(T.xn, t), tile(T.xs, t), t == 0, t == KT - 1)
+    mm.then_inc(S.mrn, 1)
+    te.wait_ge(S.ao, count(opp))
+    for k in range(HT):
+        mm = te.matmul(T.prp[0:C, 0:C], tile(T.xh, k), tile(T.xs, HT * myh + k), k == 0, k == HT - 1)
+    mm.then_inc(S.mrp, 1)
+    for a in arrivals[:-1]:
+        far_product(a)
+    te.wait_ge(S.idn, 1)
+    te.wait_ge(S.vrn, 1)
+    te.matmul(T.pkn[0:C, 0:C], T.ret[0:C, 0:C], T.idn[0:C, :], True, True).then_inc(S.mkn, 1)
+    te.wait_ge(S.vrp, 1)
+    te.matmul(T.pkp[0:C, 0:C], T.ret[0:C, C:2 * C], T.idn[0:C, :], True, True).then_inc(S.mkp, 1)
+    far_product(arrivals[-1])
+
     ve = g.vector
-    ve.memset(T.ret[C:2 * C, :], 0.0).then_inc(S.ms, 1)
-    ve.memset(T.ys[0:C, blk(core)], 0.0).then_inc(S.vys, 1)
-    nys = 1
-    ve.wait_ge(S.mrn, 1)
-    ve.tensor_copy(T.ret[0:C, 0:C], T.prn[0:C, 0:C]).then_inc(S.vrn, 1)
-    ve.wait_ge(S.mkn, 1)
-    ve.tensor_copy(T.ys[0:C, blk(nxt)], T.pkn[0:C, 0:C]).then_inc(S.vys, 1)
-    nys += 1
-    ve.wait_ge(S.mrp, 1)
-    ve.tensor_copy(T.ret[0:C, C:2 * C], T.prp[0:C, 0:C]).then_inc(S.vrp, 1)
-    for (turn, j, s, cnt) in arrivals:
+    nys = [0]
+
+    def far_copy(a):
+        (step, j, s, cnt) = a
         ve.wait_ge(S["mc%d" % j], 1)
         ve.tensor_copy(T.ys[0:C, blk(s)], T["pc%d" % j][0:C, 0:C]).then_inc(S.vys, 1)
-        nys += 1
+        nys[0] += 1
+
+    ve.memset(T.idn[0:C, :], 1.0).then_inc(S.ms1, 1)
+    ve.memset(T.ret[C:2 * C, :], 0.0).then_inc(S.ms, 1)
+    ve.memset(T.ys[0:C, blk(core)], 0.0).then_inc(S.vys, 1)
+    nys[0] += 1
+    ve.wait_ge(S.mrn, 1)
+    ve.tensor_copy(T.ret[0:C, 0:C], T.prn[0:C, 0:C]).then_inc(S.vrn, 1)
+    ve.wait_ge(S.mrp, 1)
+    ve.tensor_copy(T.ret[0:C, C:2 * C], T.prp[0:C, 0:C]).then_inc(S.vrp, 1)
+    for a in arrivals[:-1]:
+        far_copy(a)
+    ve.wait_ge(S.mkn, 1)
+    ve.tensor_copy(T.ys[0:C, blk(nxt)], T.pkn[0:C, 0:C]).then_inc(S.vys, 1)
+    nys[0] += 1
+    far_copy(arrivals[-1])
     ve.wait_ge(S.mkp, 1)
     ve.wait_ge(S.pr, count(opp))
     ve.tensor_tensor(T.ys[0:C, blk(opp)], T.pkp[0:C, 0:C], T.part[0:C, :], AluOpType.add).then_inc(S.vys, 1)
-    nys += 1
+    nys[0] += 1
 
     g.wait_ge(S.ms, 1)
     g.wait_ge(S.vrn, 1)
@@ -179,7 +210,7 @@ def rank_program(g, core, T, topo):
     write(opp, T.part[:], T.ret[:, C:2 * C], S.pr)
     g.wait_ge(S.hs, sent[0])
 
-    g.sync.wait_ge(S.vys, nys)
+    g.sync.wait_ge(S.vys, nys[0])
     g.sync.wait_ge(S.yr, count(prv))
     g.sync.dma_start(T.y[:], T.ys[0:C, :]).then_inc(S.st, 16)
     g.sync.wait_ge(S.st, 16)

@@ -7,6 +7,7 @@ W = KT * C
 H = W // 2
 HT = KT // 2
 Q = W // 4
+QT = Q // C
 XR = 128 // 4
 
 SCRATCH = {
@@ -29,8 +30,9 @@ SCRATCH = {
     "pc2": ("psum", [128, 512], "float32"),
     "pc3": ("psum", [128, 512], "float32"),
 }
-SEMAPHORES = ["ld", "ldd", "hs", "an", "ao", "c0", "c1", "c2", "c3", "yr", "pr", "mrn", "mkn", "mrp", "mkp",
-              "mc0", "mc1", "mc2", "mc3", "vrn", "vrp", "vys", "ms", "ms1", "idn", "st"]
+SEMAPHORES = (["ld", "ld0", "ld1", "hs", "an", "ao", "yr", "pr", "mrn", "mkn", "mrp", "mkp",
+               "mc0", "mc1", "mc2", "mc3", "vrn", "vrp", "vys", "vl", "vo", "ms", "ms1", "idn", "st", "st1"]
+              + ["c%d%d" % (j, u) for j in range(4) for u in range(4)])
 
 
 def _bits(mask):
@@ -79,7 +81,7 @@ def _owner_program(g, core, T, topo, rc):
         slot = T.xc[:, W * i + Q * u: W * i + Q * u + Q]
         g.wait_ge(S.ao, got)
         g.remote_dma_fused([RemoteDMATransfer(dst_ids=[_dst(topo, p, core) for p in peers], dma_engine_mask=mask,
-                                              remote_sem=S["c%d" % i], srcs=[T.xo[:]], dsts=[slot for p in peers],
+                                              remote_sem=S["c%d%d" % (i, u)], srcs=[T.xo[:]], dsts=[slot for p in peers],
                                               alu_op=0)],
                            local_sem=S.hs)
         g.wait_ge(S.hs, len(_bits(mask)))
@@ -120,29 +122,36 @@ def rank_program(g, core, T, topo):
     arrivals = []
     for j, s in enumerate(far):
         theirs = _plan(s, T, topo)[3]
-        arrivals.append((theirs[0][3].index(core), j, s, sum(count(c) for (c, q, h, peers) in theirs)))
+        seq = theirs[:1] + [e for e in theirs if e[1] == 1] + [e for e in theirs[1:] if e[1] == 0]
+        arrivals.append((theirs[0][3].index(core), j, s, [(2 * q + h, count(c)) for (c, q, h, peers) in seq]))
     arrivals.sort()
+    last = arrivals[-1][2]
 
-    g.sync.dma_start(T.xd[:], T.x[:]).then_inc(S.ldd, 16)
+    g.sync.dma_start(T.xd[0:128, :], T.x[0:XR, :]).then_inc(S.ld0, 16)
+    g.scalar.dma_start(T.xd[128:512, :], T.x[XR:128, :]).then_inc(S.ld1, 16)
     nld = 0
     for u in range(4):
-        qu = g.scalar if u % 2 == 0 else g.sync
+        qu = g.sync if u % 2 == 0 else g.scalar
         qu.dma_start(T.xs[:, Q * u: Q * u + Q], T.x[XR * u: XR * u + XR, :]).then_inc(S.ld, 16)
         nld += 16
 
     g.wait_ge(S.ms1, 1)
     g.affine_select(T.idn[0:C, :], T.idn[0:C, :], [[-1, C]], AluOpType.is_equal, 0.0, 0, 1).then_inc(S.idn, 1)
-    g.wait_ge(S.ldd, 16)
     bits = _bits(topo.mask(core, jobs[0][0]))
     per = len(bits) // len(jobs)
-    trs = []
-    for (c, q, h, peers) in jobs:
+    eng = {0: bits[0::2][:per], 1: bits[0::2][:per], 2: bits[1::2][:per], 3: bits[1::2][per:2 * per]}
+
+    def hand(job):
+        (c, q, h, peers) = job
         u = 2 * q + h
-        m = _join(bits[q::2][per * h: per * h + per])
-        trs.append(RemoteDMATransfer(dst_ids=[_dst(topo, c, core)], dma_engine_mask=m, remote_sem=S.ao,
-                                     src=T.xd[128 * u: 128 * u + 128, :], dst=T.xo[:]))
         sent[0] += per
-    g.remote_dma_fused(trs, local_sem=S.hs)
+        return RemoteDMATransfer(dst_ids=[_dst(topo, c, core)], dma_engine_mask=_join(eng[u]), remote_sem=S.ao,
+                                 src=T.xd[128 * u: 128 * u + 128, :], dst=T.xo[:])
+
+    g.wait_ge(S.ld0, 16)
+    g.remote_dma_fused([hand(jobs[0])], local_sem=S.hs)
+    g.wait_ge(S.ld1, 16)
+    g.remote_dma_fused([hand(job) for job in jobs[1:]], local_sem=S.hs)
     oh = 1 - myh
     g.wait_ge(S.ld, nld)
     write(prv, T.xn[:], T.xs[:], S.an)
@@ -151,10 +160,13 @@ def rank_program(g, core, T, topo):
     te = g.tensor
 
     def far_product(a):
-        (step, j, s, cnt) = a
-        te.wait_ge(S["c%d" % j], cnt)
-        for t in range(KT):
-            mm = te.matmul(T["pc%d" % j][0:C, 0:C], tile(T.xs, t), tile(T.xc, KT * j + t), t == 0, t == KT - 1)
+        (step, j, s, quarters) = a
+        k = 0
+        for (u, cnt) in quarters:
+            te.wait_ge(S["c%d%d" % (j, u)], cnt)
+            for t in range(QT * u, QT * u + QT):
+                mm = te.matmul(T["pc%d" % j][0:C, 0:C], tile(T.xs, t), tile(T.xc, KT * j + t), k == 0, k == KT - 1)
+                k += 1
         mm.then_inc(S["mc%d" % j], 1)
 
     te.wait_ge(S.ld, nld)
@@ -166,23 +178,22 @@ def rank_program(g, core, T, topo):
     for k in range(HT):
         mm = te.matmul(T.prp[0:C, 0:C], tile(T.xh, k), tile(T.xs, HT * myh + k), k == 0, k == HT - 1)
     mm.then_inc(S.mrp, 1)
-    for a in arrivals[:-1]:
-        far_product(a)
     te.wait_ge(S.idn, 1)
     te.wait_ge(S.vrn, 1)
     te.matmul(T.pkn[0:C, 0:C], T.ret[0:C, 0:C], T.idn[0:C, :], True, True).then_inc(S.mkn, 1)
+    far_product(arrivals[0])
     te.wait_ge(S.vrp, 1)
     te.matmul(T.pkp[0:C, 0:C], T.ret[0:C, C:2 * C], T.idn[0:C, :], True, True).then_inc(S.mkp, 1)
-    far_product(arrivals[-1])
+    for a in arrivals[1:]:
+        far_product(a)
 
     ve = g.vector
     nys = [0]
 
-    def far_copy(a):
-        (step, j, s, cnt) = a
+    def far_copy(a, sem):
+        (step, j, s, quarters) = a
         ve.wait_ge(S["mc%d" % j], 1)
-        ve.tensor_copy(T.ys[0:C, blk(s)], T["pc%d" % j][0:C, 0:C]).then_inc(S.vys, 1)
-        nys[0] += 1
+        ve.tensor_copy(T.ys[0:C, blk(s)], T["pc%d" % j][0:C, 0:C]).then_inc(sem, 1)
 
     ve.memset(T.idn[0:C, :], 1.0).then_inc(S.ms1, 1)
     ve.memset(T.ret[C:2 * C, :], 0.0).then_inc(S.ms, 1)
@@ -192,16 +203,16 @@ def rank_program(g, core, T, topo):
     ve.tensor_copy(T.ret[0:C, 0:C], T.prn[0:C, 0:C]).then_inc(S.vrn, 1)
     ve.wait_ge(S.mrp, 1)
     ve.tensor_copy(T.ret[0:C, C:2 * C], T.prp[0:C, 0:C]).then_inc(S.vrp, 1)
-    for a in arrivals[:-1]:
-        far_copy(a)
     ve.wait_ge(S.mkn, 1)
     ve.tensor_copy(T.ys[0:C, blk(nxt)], T.pkn[0:C, 0:C]).then_inc(S.vys, 1)
     nys[0] += 1
-    far_copy(arrivals[-1])
+    for a in arrivals[:-1]:
+        far_copy(a, S.vys)
+        nys[0] += 1
     ve.wait_ge(S.mkp, 1)
     ve.wait_ge(S.pr, count(opp))
-    ve.tensor_tensor(T.ys[0:C, blk(opp)], T.pkp[0:C, 0:C], T.part[0:C, :], AluOpType.add).then_inc(S.vys, 1)
-    nys[0] += 1
+    ve.tensor_tensor(T.ys[0:C, blk(opp)], T.pkp[0:C, 0:C], T.part[0:C, :], AluOpType.add).then_inc(S.vo, 1)
+    far_copy(arrivals[-1], S.vl)
 
     g.wait_ge(S.ms, 1)
     g.wait_ge(S.vrn, 1)
@@ -210,7 +221,22 @@ def rank_program(g, core, T, topo):
     write(opp, T.part[:], T.ret[:, C:2 * C], S.pr)
     g.wait_ge(S.hs, sent[0])
 
+    late = sorted([blk(opp).start, blk(last).start])
+    runs, a = [], 0
+    for b in late + [8 * C]:
+        if b > a:
+            runs.append((a, b))
+        a = b + C
     g.sync.wait_ge(S.vys, nys[0])
     g.sync.wait_ge(S.yr, count(prv))
-    g.sync.dma_start(T.y[:], T.ys[0:C, :]).then_inc(S.st, 16)
-    g.sync.wait_ge(S.st, 16)
+    nst = 0
+    for (a, b) in runs:
+        g.sync.dma_start(T.y[:, a:b], T.ys[0:C, a:b]).then_inc(S.st, 16)
+        nst += 16
+    g.sync.wait_ge(S.vo, 1)
+    g.sync.dma_start(T.y[:, blk(opp)], T.ys[0:C, blk(opp)]).then_inc(S.st, 16)
+    nst += 16
+    g.sync.wait_ge(S.st, nst)
+    g.scalar.wait_ge(S.vl, 1)
+    g.scalar.dma_start(T.y[:, blk(last)], T.ys[0:C, blk(last)]).then_inc(S.st1, 16)
+    g.scalar.wait_ge(S.st1, 16)

from concourse.bass import DstId, RemoteDMATransfer
from concourse.mybir import AluOpType

SIM_CORES = 256
KT, C = 8, 64
W = KT * C
H = W // 2
HT = KT // 2
Q = W // 4
QT = Q // C
XR = 128 // 4

SCRATCH = {
    "xd": ("dram", [512, Q], "bfloat16"),
    "xo": ("dram", [128, Q], "bfloat16"),
    "xs": ("sbuf", [128, W], "bfloat16"),
    "xn": ("sbuf", [128, W], "bfloat16"),
    "xh": ("sbuf", [128, H], "bfloat16"),
    "xc": ("sbuf", [128, 4 * W], "bfloat16"),
    "idn": ("sbuf", [128, C], "bfloat16"),
    "ys": ("sbuf", [128, 8 * C], "bfloat16"),
    "ret": ("sbuf", [128, 2 * C], "bfloat16"),
    "part": ("sbuf", [128, C], "bfloat16"),
    "prn": ("psum", [128, 512], "float32"),
    "pkn": ("psum", [128, 512], "float32"),
    "prp": ("psum", [128, 512], "float32"),
    "pkp": ("psum", [128, 512], "float32"),
    "pc0": ("psum", [128, 512], "float32"),
    "pc1": ("psum", [128, 512], "float32"),
    "pc2": ("psum", [128, 512], "float32"),
    "pc3": ("psum", [128, 512], "float32"),
}
SEMAPHORES = (["ld", "ld0", "ld1", "hs", "an", "ao", "yr", "pr", "mrn", "mkn", "mrp", "mkp",
               "mc0", "mc1", "mc2", "mc3", "vrn", "vrp", "vys", "vl", "vo", "ms", "ms1", "idn", "st", "st1"]
              + ["c%d%d" % (j, u) for j in range(4) for u in range(4)])


def _bits(mask):
    return [1 << b for b in range(mask.bit_length()) if (mask >> b) & 1]


def _join(bits):
    m = 0
    for b in bits:
        m |= b
    return m


def _dst(topo, dst, src):
    rid, pid = topo.addr(dst, src)
    return DstId(rid=rid, pnc=pid)


def _plan(rc, T, topo):
    own = [c for c in T.cores if c == rc or topo.same_plane(c, rc)]
    far = [c for c in T.cores if c not in own]
    i = own.index(rc)
    chip = [c for c in range(SIM_CORES) if topo.host(c) == topo.host(rc) and topo.chip(c) == topo.chip(rc)]
    owners = [c for c in chip if c != rc and topo.may_write(c, far[0])]
    near = [c for c in owners if topo.die(c) == topo.die(rc)]
    away = [c for c in owners if topo.die(c) != topo.die(rc)]
    peers = [far[(i + k) % len(far)] for k in range(len(far))]
    jobs = []
    for q, grp in enumerate((near, away)):
        for h, c in enumerate(grp[:2]):
            jobs.append((c, q, h, peers))
    return own, far, i, jobs


def _owner_program(g, core, T, topo, rc):
    S = T.sem
    own, far, i, jobs = _plan(rc, T, topo)
    for (c, q, h, peers) in jobs:
        if c != core:
            continue
        u = 2 * q + h
        got = len(_bits(topo.mask(rc, core))) // len(jobs)
        mask = topo.mask(core, peers[0])
        for p in peers:
            mask &= topo.mask(core, p)
        slot = T.xc[:, W * i + Q * u: W * i + Q * u + Q]
        g.wait_ge(S.ao, got)
        g.remote_dma_fused([RemoteDMATransfer(dst_ids=[_dst(topo, p, core) for p in peers], dma_engine_mask=mask,
                                              remote_sem=S["c%d%d" % (i, u)], srcs=[T.xo[:]], dsts=[slot for p in peers],
                                              alu_op=0)],
                           local_sem=S.hs)
        g.wait_ge(S.hs, len(_bits(mask)))


def rank_program(g, core, T, topo):
    S = T.sem
    rank = T.rank_of(core)
    if rank is None:
        home = [c for c in T.cores if topo.host(c) == topo.host(core) and topo.chip(c) == topo.chip(core)]
        if home:
            _owner_program(g, core, T, topo, home[0])
        return

    own, far, i, jobs = _plan(core, T, topo)
    n = len(own)
    nxt, prv, opp = own[(i + 1) % n], own[(i - 1) % n], own[(i + 2) % n]
    myh = 0 if i < n // 2 else 1
    sent = [0]

    def blk(c):
        k = T.rank_of(c)
        return slice(C * k, C * k + C)

    def tile(buf, t):
        return buf[:, C * t: C * t + C]

    def count(src):
        return len(_bits(topo.mask(src, core)))

    def write(d, out_ap, in_ap, sem):
        m = topo.mask(core, d)
        rid, pid = topo.addr(d, core)
        g.remote_dma(out_ap=out_ap, in_ap=in_ap, remote_sem=sem, local_sem=S.hs, pid=pid, routing_id=rid,
                     dma_engine_mask=m)
        sent[0] += len(_bits(m))

    arrivals = []
    for j, s in enumerate(far):
        theirs = _plan(s, T, topo)[3]
        seq = theirs[:1] + [e for e in theirs if e[1] == 1] + [e for e in theirs[1:] if e[1] == 0]
        arrivals.append((theirs[0][3].index(core), j, s, [(2 * q + h, count(c)) for (c, q, h, peers) in seq]))
    arrivals.sort()
    last = arrivals[-1][2]

    g.sync.dma_start(T.xd[0:128, :], T.x[0:XR, :]).then_inc(S.ld0, 16)
    g.scalar.dma_start(T.xd[128:512, :], T.x[XR:128, :]).then_inc(S.ld1, 16)
    nld = 0
    for u in range(4):
        qu = g.sync if u % 2 == 0 else g.scalar
        qu.dma_start(T.xs[:, Q * u: Q * u + Q], T.x[XR * u: XR * u + XR, :]).then_inc(S.ld, 16)
        nld += 16

    g.wait_ge(S.ms1, 1)
    g.affine_select(T.idn[0:C, :], T.idn[0:C, :], [[-1, C]], AluOpType.is_equal, 0.0, 0, 1).then_inc(S.idn, 1)
    bits = _bits(topo.mask(core, jobs[0][0]))
    per = len(bits) // len(jobs)
    eng = {0: bits[0::2][:per], 1: bits[0::2][:per], 2: bits[1::2][:per], 3: bits[1::2][per:2 * per]}

    def hand(job):
        (c, q, h, peers) = job
        u = 2 * q + h
        sent[0] += per
        return RemoteDMATransfer(dst_ids=[_dst(topo, c, core)], dma_engine_mask=_join(eng[u]), remote_sem=S.ao,
                                 src=T.xd[128 * u: 128 * u + 128, :], dst=T.xo[:])

    g.wait_ge(S.ld0, 16)
    g.remote_dma_fused([hand(jobs[0])], local_sem=S.hs)
    g.wait_ge(S.ld1, 16)
    g.remote_dma_fused([hand(job) for job in jobs[1:]], local_sem=S.hs)
    oh = 1 - myh
    g.wait_ge(S.ld, nld)
    write(prv, T.xn[:], T.xs[:], S.an)
    write(opp, T.xh[:], T.xs[:, H * oh: H * oh + H], S.ao)

    te = g.tensor

    def far_product(a):
        (step, j, s, quarters) = a
        k = 0
        for (u, cnt) in quarters:
            te.wait_ge(S["c%d%d" % (j, u)], cnt)
            for t in range(QT * u, QT * u + QT):
                mm = te.matmul(T["pc%d" % j][0:C, 0:C], tile(T.xs, t), tile(T.xc, KT * j + t), k == 0, k == KT - 1)
                k += 1
        mm.then_inc(S["mc%d" % j], 1)

    te.wait_ge(S.ld, nld)
    te.wait_ge(S.an, count(nxt))
    for t in range(KT):
        mm = te.matmul(T.prn[0:C, 0:C], tile(T.xn, t), tile(T.xs, t), t == 0, t == KT - 1)
    mm.then_inc(S.mrn, 1)
    te.wait_ge(S.ao, count(opp))
    for k in range(HT):
        mm = te.matmul(T.prp[0:C, 0:C], tile(T.xh, k), tile(T.xs, HT * myh + k), k == 0, k == HT - 1)
    mm.then_inc(S.mrp, 1)
    te.wait_ge(S.idn, 1)
    te.wait_ge(S.vrn, 1)
    te.matmul(T.pkn[0:C, 0:C], T.ret[0:C, 0:C], T.idn[0:C, :], True, True).then_inc(S.mkn, 1)
    far_product(arrivals[0])
    te.wait_ge(S.vrp, 1)
    te.matmul(T.pkp[0:C, 0:C], T.ret[0:C, C:2 * C], T.idn[0:C, :], True, True).then_inc(S.mkp, 1)
    for a in arrivals[1:]:
        far_product(a)

    ve = g.vector
    nys = [0]

    def far_copy(a, sem):
        (step, j, s, quarters) = a
        ve.wait_ge(S["mc%d" % j], 1)
        ve.tensor_copy(T.ys[0:C, blk(s)], T["pc%d" % j][0:C, 0:C]).then_inc(sem, 1)

    ve.memset(T.idn[0:C, :], 1.0).then_inc(S.ms1, 1)
    ve.memset(T.ret[C:2 * C, :], 0.0).then_inc(S.ms, 1)
    ve.memset(T.ys[0:C, blk(core)], 0.0).then_inc(S.vys, 1)
    nys[0] += 1
    ve.wait_ge(S.mrn, 1)
    ve.tensor_copy(T.ret[0:C, 0:C], T.prn[0:C, 0:C]).then_inc(S.vrn, 1)
    ve.wait_ge(S.mrp, 1)
    ve.tensor_copy(T.ret[0:C, C:2 * C], T.prp[0:C, 0:C]).then_inc(S.vrp, 1)
    ve.wait_ge(S.mkn, 1)
    ve.tensor_copy(T.ys[0:C, blk(nxt)], T.pkn[0:C, 0:C]).then_inc(S.vys, 1)
    nys[0] += 1
    for a in arrivals[:-1]:
        far_copy(a, S.vys)
        nys[0] += 1
    ve.wait_ge(S.mkp, 1)
    ve.wait_ge(S.pr, count(opp))
    ve.tensor_tensor(T.ys[0:C, blk(opp)], T.pkp[0:C, 0:C], T.part[0:C, :], AluOpType.add).then_inc(S.vo, 1)
    far_copy(arrivals[-1], S.vl)

    g.wait_ge(S.ms, 1)
    g.wait_ge(S.vrn, 1)
    write(nxt, T.ys[:, blk(core)], T.ret[:, 0:C], S.yr)
    g.wait_ge(S.vrp, 1)
    write(opp, T.part[:], T.ret[:, C:2 * C], S.pr)
    g.wait_ge(S.hs, sent[0])

    late = sorted([blk(opp).start, blk(last).start])
    runs, a = [], 0
    for b in late + [8 * C]:
        if b > a:
            runs.append((a, b))
        a = b + C
    g.sync.wait_ge(S.vys, nys[0])
    g.sync.wait_ge(S.yr, count(prv))
    nst = 0
    for (a, b) in runs:
        g.sync.dma_start(T.y[:, a:b], T.ys[0:C, a:b]).then_inc(S.st, 16)
        nst += 16
    g.sync.wait_ge(S.vo, 1)
    g.sync.dma_start(T.y[:, blk(opp)], T.ys[0:C, blk(opp)]).then_inc(S.st, 16)
    nst += 16
    g.sync.wait_ge(S.st, nst)
    g.scalar.wait_ge(S.vl, 1)
    g.scalar.dma_start(T.y[:, blk(last)], T.ys[0:C, blk(last)]).then_inc(S.st1, 16)
    g.scalar.wait_ge(S.st1, 16)
